import numpy as np, ml_dtypes
CORES = [36,164,52,180,100,228,116,244]
N = 8
BF = ml_dtypes.bfloat16
def gentries(a):
    return np.ascontiguousarray(a.reshape(8, 16, -1).transpose(0, 2, 1)).reshape(8, -1)
def gtable(e):
    e = np.asarray(e); return np.ascontiguousarray(e.reshape(8, -1, 16).transpose(0, 2, 1)).reshape(128, -1).astype(np.int32)
def f(rng, *shape):
    return (rng.standard_normal(shape, dtype=np.float32) * np.exp2(rng.integers(-2, 3, shape[:-1] + (1,)))).astype(BF)
def wide(rng, *shape):
    v = f(rng, *shape).astype(np.float32); k = shape[:-2] + (1, shape[-1])
    return (v * np.exp2(rng.integers(-6, 7, k)) * (rng.random(k) > 0.0625)).astype(BF)
V, G, E, C, M, H = 1216, 128, 6, 4, 336, 48
ORDER = [0, 1, 2, 3, 0, 1, 2, 3]
W = V + (N - 1) * G
def ghosts(z, S):
    for r in range(N):
        for d in range(N - 1):
            s = (r + 1 + d) % N
            z[r, :, :, V + d * G:V + (d + 1) * G] = np.take_along_axis(z[s, :, :, :V], S[s][:, N - 2 - d][:, None, :], 2)
def halos(halo):
    return np.stack([gentries(v) for v in halo]).reshape(N, 8, N - 1, G).astype(np.int64)
def around(hue, S):
    w = np.zeros((N, 8, 1, W), np.int64); w[:, :, 0, :V] = hue; ghosts(w, S); return w[:, :, 0]
def counts(rng, n, cap, fill):
    if rng.random() < fill: return rng.permutation(np.minimum(np.maximum(n - cap * np.arange(C), 0), cap))
    return np.bincount(rng.permutation(np.repeat(np.arange(C), cap))[:n], minlength=C)
def single(rng, v):
    return v.astype(np.float32) * (rng.random(v.shape, dtype=np.float32) + np.float32(0.5))
def make(rng, fill, rep, lo):
    hue = np.zeros((N, 8, V), np.int32); S = np.zeros((N, 8, N - 1, G), np.int64); nb = np.zeros((N, 8, E, V), np.int32)
    for r in range(N):
        for g in range(8):
            n = counts(rng, V, M, fill); o = rng.permutation(C); h = np.repeat(o, n[o])
            if not rep: h = rng.permutation(h)
            hue[r, g] = h; own = [np.flatnonzero(h == c) for c in range(C)]
            for d in range(N - 1):
                n = counts(rng, G, H, fill)
                S[r, g, d] = rng.permutation(np.concatenate([own[c][-rng.integers(0, 2, n[c])] if rep else rng.permutation(own[c])[:n[c]] for c in range(C)]))
    w = around(hue, S)
    for r in range(N):
        for g in range(8):
            k = w[r, g, lo:]; o = np.argsort(k, kind="stable"); n = np.bincount(k, minlength=C); a = np.add.accumulate(n) - n; c = hue[r, g]
            u = rng.integers(0, (len(k) - n[c])[None, :], (E, V)); u = u + n[c] * (u >= a[c]); p = lo + o[u]
            if rep:
                p[3:] = p[2]; p[0] = np.where(c != w[r, g, 0], 0, p[0]); p[1] = np.where(c != w[r, g, W - 1], W - 1, p[1])
            nb[r, g] = p
    co = (rng.random((N, 8, E * V)) - 0.5) * 0.5
    if rep: co = co * (rng.random(co.shape) > 0.25)
    return {"x": single(rng, f(rng, N, 128, V)), "b": f(rng, N, 128, V), "nb": nb.reshape(N, 8, E * V), "co": co.astype(np.float32).astype(BF), "di": (0.5 + 0.5 * rng.random((N, 8, V))).astype(np.float32),
            "hue": hue, "halo": np.stack([gtable(S[r].reshape(8, -1)) for r in range(N)])}
def setup_inputs(rng):
    return make(rng, 0.25, False, 0)
def setup_inputs_full(rng):
    return make(rng, 2.0, False, 0)
def setup_inputs_repeats(rng):
    return make(rng, 0.5, True, 0)
def setup_inputs_ghosts(rng):
    return make(rng, 0.25, False, V)
def setup_inputs_spread(rng):
    d = make(rng, 0.25, False, 0); d["x"] = single(rng, wide(rng, N, 128, V)); d["b"] = wide(rng, N, 128, V); return d
def check_inputs(d):
    bad = []; hue, nb, S = d["hue"], d["nb"], halos(d["halo"])
    if hue.min() < 0 or hue.max() >= C: bad.append("colours")
    if S.min() < 0 or S.max() >= V: bad.append("halo")
    if nb.min() < 0 or nb.max() >= W: bad.append("places")
    if not (np.abs(d["x"]) <= 2.0 ** 30).all() or not (np.abs(d["b"].astype(np.float32)) <= 2.0 ** 30).all(): bad.append("sizes")
    if not (np.abs(d["co"].astype(np.float32)) <= 0.5).all(): bad.append("coefficients")
    if not ((d["di"] > 0) & (d["di"] <= 1)).all(): bad.append("diagonals")
    if bad: return bad
    w = around(hue, S); q = w[:, :, V:].reshape(N, 8, N - 1, G)
    if max(np.count_nonzero(hue == c, axis=2).max() for c in range(C)) > M: bad.append("vertices of a colour")
    if max(np.count_nonzero(q == c, axis=3).max() for c in range(C)) > H: bad.append("halo entries of a colour")
    if (np.take_along_axis(w, nb.astype(np.int64), 2).reshape(N, 8, E, V) == hue[:, :, None]).any(): bad.append("neighbours")
    return bad
def reference(x, b, nb, co, di, hue, halo):
    S = halos(halo); P = nb.reshape(N, 8, E, V); A = co.astype(np.float64).reshape(N, 8, E, V); D = di.astype(np.float64); R = b.astype(np.float64).reshape(N, 8, 16, V)
    z = np.zeros((N, 8, 16, W), np.float64); z[..., :V] = x.reshape(N, 8, 16, V); ghosts(z, S)
    for c in ORDER:
        for r in range(N):
            for g in range(8):
                v = np.flatnonzero(hue[r, g] == c); s = np.zeros((16, len(v)), np.float64)
                for e in range(E): s += A[r, g, e, v] * z[r, g][:, P[r, g, e, v]]
                z[r, g][:, v] = D[r, g, v] * (R[r, g][:, v] - s)
        ghosts(z, S)
    return {"y": z[..., :V].reshape(N, 128, V).astype(np.float32)}

from concourse.bass import DstId, RemoteDMATransfer
from concourse.mybir import AluOpType, ActivationFunctionType

N, V, G, E, C, M = 8, 1216, 128, 6, 4, 336
ORDER = [0, 1, 2, 3, 0, 1, 2, 3]
NG = (N - 1) * G
Z0 = M
ZG = Z0 + V
ZW = ZG + NG
EM = E * M
LC = EM // 16
PC = 22
BANK = 512
VH = V // 2
JW = 160
W0, W1 = 152, 576
SU0, HL0 = 3 * LC + 3 * PC, 3 * LC + 3 * PC + 76
VCH = [(0, 64), (64, 149), (149, 252), (252, 336)]
PLAN = [("v", 0, 192), ("a", 192, 384), ("a", 384, 896), ("a", 896, 1536), ("a", 1760, 2016), ("m", 0, 384), ("p", 0), ("v", 1536, 1760), ("m", 384, 512), ("m", 512, 896), ("p", 1), ("f", 0), ("m", 896, 1024), ("m", 1024, 1536), ("p", 2), ("m", 1536, 2016), ("s", 3), ("f", 1), ("f", 2)]
PLAN0 = [("a", 0, 384), ("a", 384, 896), ("a", 896, 1536), ("a", 1536, 2016), ("m", 0, 384), ("p", 0), ("d",), ("m", 384, 512), ("m", 512, 896), ("p", 1), ("f", 0), ("m", 896, 1024), ("m", 1024, 1536), ("p", 2), ("m", 1536, 2016), ("s", 3), ("f", 1), ("f", 2)]
TABLES = {"di": (16, "float32", 0), "x0": (76, "float32", None), "co": (57, "bfloat16", 0), "b": (152, "bfloat16", 0), "x1": (76, "float32", None), "hu": (7, "uint16", None), "l0": (W0 // 8, "uint16", None), "l1": (W1 // 8, "uint16", None)}
DR = V // 16
YP = [(0, 320, 0), (320, 768, None), (768, 1216, None)]

SCRATCH = {}
for _n, (_w, _t, _h) in TABLES.items():
    SCRATCH["st_" + _n] = ("dram", [N * DR, _w] if _n == "di" else [N, 128, _w], _t)
    SCRATCH["ld_" + _n] = ("dram", [N, 128, _w], _t)
for _k, (_a, _b, _h) in enumerate(YP):
    SCRATCH["st_y%d" % _k] = ("dram", [N, 128, (_b - _a) // 8], "float32")
    SCRATCH["ld_y%d" % _k] = ("dram", [N, 128, (_b - _a) // 8], "float32")
for _k in range(8):
    SCRATCH["P%d" % _k] = ("psum", [128, BANK], "float32")
for _n, _w, _t in [
        ("J2", 256, "float32"), ("J16", JW, "float16"), ("IB", 128, "bfloat16"),
        ("BO", 128, "float32"), ("BO1", 128, "float32"), ("TR", 128, "float32"), ("BOB", 128, "bfloat16"), ("NTB", 128, "bfloat16"),
        ("BE", E * 128, "bfloat16"), ("E8", 128, "float32"), ("SM", 6 * JW, "float16"), ("W6", 256, "float32"),
        ("KI", 8, "int32"), ("KJ", 8, "int32"), ("KF", 8, "float32"), ("I16", 16, "float32"), ("LT", 16, "float32"), ("MN", 16, "float32"),
        ("MR", 8, "float32"), ("CP", 304, "bfloat16"), ("C336", 304, "bfloat16"), ("RM", 304, "bfloat16"), ("SC", BANK, "float32"),
        ("HI", 128, "int32"), ("HB", 128, "bfloat16"), ("MS", 304, "bfloat16"), ("SS", 304, "bfloat16"), ("TT", 304, "float32"),
        ("UU", 152, "float32"), ("SF", 76, "float32"), ("SH", 76, "float16"),
        ("NBI", V, "int32"), ("NS", C * M, "float32"), ("NH", C * M, "float16"),
        ("HA", 56, "int32"), ("HU", 56, "uint16"), ("HD", 56, "uint16"), ("SR", V, "float32"), ("HS", NG, "float32"),
        ("LS0", W0, "uint16"), ("LS1", W1, "uint16"), ("LD0", W0, "uint16"), ("LD1", W1, "uint16"),
        ("D8", V, "float32"), ("DW", ZG, "float32"), ("CW", ZG, "bfloat16"), ("BW", ZG, "bfloat16"),
        ("DS", C * M, "float32"), ("CS", C * M, "bfloat16"), ("BS", C * M, "bfloat16"),
        ("Z", ZW, "float32"), ("R", C * M, "float32"), ("ZN", EM, "float32"), ("PR", EM, "float32"),
        ("HH", NG, "float32"), ("Y", V, "float32")]:
    SCRATCH[_n] = ("sbuf", [128, _w], _t)

SEMAPHORES = ["cv", "ca", "cp", "cg", "sent", "o_x0", "o_x1", "o_di", "o_b", "l_hue", "l_nb", "l_ha", "l_own"]
for _n in list(TABLES) + ["y%d" % _k for _k in range(len(YP))]:
    SEMAPHORES += ["s_" + _n, "a_" + _n, "h_" + _n, "l_" + _n]


def helpers_of(core, topo):
    return [c for c in topo.cores_of(core) if topo.die(c) != topo.die(core)]


def di_first(k):
    return min(DR * k, N * DR - 128)


def send_slots(g, T, topo, core, me, name, via, relay):
    trs = []
    for e in range(N - 1):
        k = (me + 1 + e) % N
        off = topo.engines(core, T.cores[k])
        if relay:
            src = T["ld_" + name][k]
        elif name == "di":
            src = T.st_di[di_first(k):di_first(k) + 128, :]
        else:
            src = T["st_" + name][k]
        if via is None:
            dst, ap, sem, eng = T.cores[k], T["ld_" + name][me], T.sem["a_" + name], off[e]
        else:
            rest = [q for q in topo.engines(core, via) if q not in off]
            dst, ap, sem, eng = via, T["ld_" + name][k], T.sem["h_" + name], rest[e]
        rid, pid = topo.addr(dst, core)
        trs.append(RemoteDMATransfer(dst_ids=[DstId(rid=rid, pnc=pid)], dma_engine_mask=1 << eng, remote_sem=sem, src=src, dst=ap))
    return g.remote_dma_fused(trs, local_sem=T.sem.sent)


def helper_program(g, core, T, topo):
    routes = [(n, h) for n, (w, t, h) in TABLES.items()] + [("y%d" % k, h) for k, (a, b, h) in enumerate(YP)]
    for r, rc in enumerate(T.cores):
        hs = helpers_of(rc, topo)
        if core not in hs:
            continue
        n = 0
        for name, h in routes:
            if h is not None and hs[h] == core:
                g.wait_ge(T.sem["h_" + name], N - 1)
                send_slots(g, T, topo, core, r, name, None, True)
                n += N - 1
        if n:
            g.wait_ge(T.sem.sent, n)


def emit(g, T, ops):
    Q = {"v": g.vector, "a": g.scalar, "p": g.tensor, "g": g, "s": g.sync}
    hist = {}
    for i, o in enumerate(ops):
        deps = set()
        for kind, regs in (("r", o["r"]), ("w", o["w"])):
            for (b, lo, hi) in regs:
                psum = SCRATCH[b][0] == "psum"
                for (j, k2, lo2, hi2) in hist.get(b, []):
                    p = ops[j]
                    if p["remote"] or (p["sem"] is not None and p["sem"] == o["sem"]):
                        continue
                    if (psum and p["q"] != o["q"]) or (lo < hi2 and lo2 < hi and (kind == "w" or k2 == "w")):
                        deps.add(j)
        for kind, regs in (("r", o["r"]), ("w", o["w"])):
            for (b, lo, hi) in regs:
                hist.setdefault(b, []).append((i, kind, lo, hi))
        o["deps"] = deps
    total = {}
    for o in ops:
        if o["sem"] is not None:
            total[o["sem"]] = total.get(o["sem"], 0) + 16 * len(o["f"])
    pos, known, group_clock = {}, {q: {} for q in Q}, {}
    for o in ops:
        kn = known[o["q"]]
        waits = []
        for j in sorted(o["deps"], reverse=True):
            p = ops[j]
            key, val = (p["sem"], 1) if p["sem"] is not None else ("c" + p["q"], p["pos"])
            if kn.get(key, 0) >= val:
                continue
            waits.append(j)
            kn[key] = val
            for k2, v2 in (group_clock[p["sem"]] if p["sem"] is not None else p["clock"]).items():
                if kn.get(k2, 0) < v2:
                    kn[k2] = v2
        o["waits"] = waits
        pos[o["q"]] = pos.get(o["q"], 0) + 1
        o["pos"] = pos[o["q"]]
        o["clock"] = dict(kn)
        if o["sem"] is not None:
            clock = group_clock.setdefault(o["sem"], {})
            for k2, v2 in kn.items():
                if clock.get(k2, 0) < v2:
                    clock[k2] = v2
    dep_any = set()
    for o in ops:
        dep_any |= o["deps"]
    count, waited, sent = {}, {}, 0
    for i, o in enumerate(ops):
        q = Q[o["q"]]
        for (s, v) in o["after"]:
            q.wait_ge(T.sem[s], v)
        for j in o["waits"]:
            p = ops[j]
            s, v = (p["sem"], total[p["sem"]]) if p["sem"] is not None else ("c" + p["q"], p["count"])
            q.wait_ge(T.sem[s], v)
            waited[s] = max(waited.get(s, 0), v)
        for f in o["f"]:
            ins = f()
            if o["remote"]:
                sent += N - 1
            elif o["sem"] is not None:
                ins.then_inc(T.sem[o["sem"]], 16)
            elif i in dep_any:
                ins.then_inc(T.sem["c" + o["q"]], 1)
                count["c" + o["q"]] = count.get("c" + o["q"], 0) + 1
        o["count"] = count.get("c" + o["q"], 0)
    g.wait_ge(T.sem.sent, sent)
    for s, v in list(total.items()) + list(count.items()):
        if waited.get(s, 0) < v:
            g.sync.wait_ge(T.sem[s], v)


def rank_program(g, core, T, topo):
    me = T.rank_of(core)
    if me is None:
        helper_program(g, core, T, topo)
        return
    A = AluOpType
    COPY = ActivationFunctionType.Copy
    ops = []
    hs = helpers_of(core, topo)

    def op(q, f, r=(), w=(), sem=None, after=(), remote=False):
        ops.append({"q": q, "f": f if isinstance(f, list) else [f], "r": list(r), "w": list(w), "sem": sem,
                    "after": list(after), "remote": remote})

    def whole(b):
        return (b, 0, 1 << 20)

    def dma(q, out, in_, sem, r=(), w=(), after=()):
        e = g.sync if q == "s" else g.scalar
        op(q, lambda: e.dma_start(out, in_), r, w, sem, after)

    def send(name, h):
        op("g", lambda: send_slots(g, T, topo, core, me, name, None if h is None else hs[h], False), [whole("st_" + name)], remote=True)

    def memset(b, lo, hi, val, step=1):
        op("v", lambda: g.vector.memset(T[b][:, lo:hi:step], val), w=[(b, lo, hi)])

    def copy(q, ob, olo, ohi, ib, ilo, ihi, scale=None, rs=()):
        if q == "v":
            f = lambda: g.vector.tensor_copy(T[ob][:, olo:ohi], T[ib][:, ilo:ihi])
        elif scale is None:
            f = lambda: g.scalar.activation(T[ob][:, olo:ohi], T[ib][:, ilo:ihi], COPY)
        else:
            f = lambda: g.scalar.activation(T[ob][:, olo:ohi], T[ib][:, ilo:ihi], COPY, scale=scale)
        op(q, f, [(ib, ilo, ihi)] + list(rs), [(ob, olo, ohi)])

    def gather(q, ob, olo, wb, wlo, whi, lb, llo, lhi):
        ohi = olo + 16 * (lhi - llo)
        if q == "v":
            f = lambda: g.vector.tensor_copy(T[ob][:, olo:ohi], T[wb][:, wlo:whi].indirect(T[lb][:, llo:lhi]))
        else:
            f = lambda: g.scalar.activation(T[ob][:, olo:ohi], T[wb][:, wlo:whi].indirect(T[lb][:, llo:lhi]), COPY)
        op(q, f, [(wb, wlo, whi), (lb, llo, lhi)], [(ob, olo, ohi)])

    def scatter(wb, wlo, whi, lb, llo, lhi, ib, ilo):
        ihi = ilo + 16 * (lhi - llo)
        op("v", lambda: g.vector.tensor_copy(T[wb][:, wlo:whi].indirect(T[lb][:, llo:lhi]), T[ib][:, ilo:ihi]),
           [(ib, ilo, ihi), (lb, llo, lhi)], [(wb, wlo, whi)])

    def tt(o, a, b, alu):
        op("v", lambda: g.vector.tensor_tensor(T[o[0]][:, o[1]:o[2]:o[3]], T[a[0]][:, a[1]:a[2]:a[3]], T[b[0]][:, b[1]:b[2]:b[3]], alu),
           [a[:3], b[:3]], [o[:3]])

    def ts(o, a, s, alu, rs=()):
        op("v", lambda: g.vector.tensor_scalar(T[o[0]][:, o[1]:o[2]], T[a[0]][:, a[1]:a[2]], s, None, alu), [a] + list(rs), [o])

    def mm(items, r, w):
        op("p", [(lambda it=it: g.tensor.matmul(it[0], it[1], it[2], it[3], it[4])) for it in items], r, w)

    def select(ob, ib, n, pat, cmp, base, cm, parts=128):
        op("g", lambda: g.affine_select(T[ob][0:parts, 0:n], T[ib][0:parts, 0:n], pat, cmp, 0.0, base, cm), [(ib, 0, n)], [(ob, 0, n)])

    def rotated(b, shift):
        o = (-shift) % 128
        return T[b][:, o:o + 128]

    def shifted(b, first, shift):
        return T[b][:, first + 16 - shift:first + 144 - shift]

    def nbl(side, c):
        return (side + "0", 0) if c == 0 else (side + "1", LC * (c - 1))

    def pul(side, c):
        return (side + "0", LC) if c == 0 else (side + "1", 3 * LC + PC * (c - 1))

    own = slice(16 * me, 16 * me + 16)
    around = [(a, b) for a, b in ((0, me), (me + 1, N)) if b > a]

    def travel(name, src, dst, q="s"):
        dma(q, T["st_" + name][:], T[src][:], "s_" + name, r=[whole(src)], w=[whole("st_" + name)])
        dma(q, T[dst][own, :], T[src][own, :], "l_" + name, r=[whole(src)], w=[whole(dst)])
        send(name, TABLES[name][2])

    def arrive(name, dst, q="s"):
        for i, (a, b) in enumerate(around):
            dma(q, T[dst][16 * a:16 * b, :], T["ld_" + name][a:b], "l_" + name, w=[whole(dst)], after=[("a_" + name, N - 1)] if i == 0 else [])

    def load_x(k):
        dma("s", T.Z[:, Z0 + VH * k:Z0 + VH * k + VH], T["ld_x%d" % k][:], "l_x%d" % k, r=[whole("ld_x%d" % k)],
            w=[("Z", Z0 + VH * k, Z0 + VH * k + VH)], after=[("a_x%d" % k, N - 1)])

    for k in range(N):
        dma("sa"[k % 2], T.HI[0:DR, 16 * k:16 * k + 16], T.hue[k], "l_hue", w=[whole("HI")])
    dma("s", T.st_di[:], T.di[:], "s_di", w=[whole("st_di")])
    dma("a", T.st_co[:], T.co[:], "s_co", w=[whole("st_co")])
    for k in range(2):
        dma("s", T["st_x%d" % k][:], T.x[:, VH * k:VH * k + VH], "s_x%d" % k, w=[whole("st_x%d" % k)])
    dma("a", T.HA[:], T.halo[:], "l_ha", w=[whole("HA")])
    dma("a", T.st_b[:], T.b[:], "s_b", w=[whole("st_b")])
    d0 = DR * me - di_first(me)
    for k in range(2):
        dma("s", T["ld_x%d" % k][me], T.x[own, VH * k:VH * k + VH], "o_x%d" % k, w=[whole("ld_x%d" % k)])
    dma("s", T.ld_di[me, d0:d0 + DR, :], T.di[me], "o_di", w=[whole("ld_di")])
    dma("s", T.ld_b[me], T.b[own, :], "o_b", w=[whole("ld_b")])

    memset("SC", 0, 256, 1.0)
    memset("SC", 256, BANK, 1.0)
    op("g", lambda: g.iota(T.KI[:, 0:1], [[0, 1]], 0, 1), w=[whole("KI")])
    op("g", lambda: g.iota(T.I16[:], [[1, 16]], 0, 0, allow_small_or_imprecise_dtypes=True), w=[whole("I16")])
    select("J2", "SC", 256, [[0, 2], [-1, 128]], A.is_equal, 0, 1)
    select("BO1", "SC", 128, [[-16, 8], [0, 16]], A.is_ge, 0, 1)
    select("BO", "BO1", 128, [[16, 8], [0, 16]], A.is_ge, 15, -1)
    select("TR", "BO", 128, [[-1, 128]], A.is_ge, 0, 1)
    for name in ("di", "x0", "co", "b", "x1"):
        send(name, TABLES[name][2])
    select("E8", "SC", 128, [[-1, 8], [0, 16]], A.is_equal, 0, 1, parts=N)
    op("v", lambda: g.vector.tensor_tensor_scan(T.NS[:, 0:M], T.SC[:, 0:M], T.SC[:, 0:M], -1.0, A.mult, A.add), [whole("SC")], [("NS", 0, M)])
    memset("RM", 0, 304, 1.0)
    for k in range(4):
        ts(("NBI", 304 * k, 304 * k + 304), ("NS", 0, 304), float(Z0 + 304 * k), A.add)
    for k in range(N):
        dma("s", T.NBI[16 * k:16 * k + E, :], T.nb[k], "l_nb", w=[whole("NBI")])
    for c in range(C):
        memset("CP", 76 * c, 76 * c + 76, float(c))
    memset("RM", 0, 304, 0.0, 76)
    copy("a", "IB", 0, 128, "J2", 0, 128)
    copy("a", "BOB", 0, 128, "BO", 0, 128)
    copy("a", "NTB", 0, 128, "TR", 0, 128, -1.0)
    for c in range(1, C):
        copy("a", "NS", M * c, M * c + M, "NS", 0, M)
    for lo in range(0, ZG, BANK):
        copy("a", "CW", lo, min(lo + BANK, ZG), "SC", 0, min(BANK, ZG - lo), 0.0)

    op("v", lambda: g.vector.tensor_copy(T.HB[0:DR, :], T.HI[0:DR, :]), [whole("HI")], [whole("HB")])
    copy("v", "HU", 0, 56, "HA", 0, 56)
    for c in range(C):
        memset("C336", 76 * c, 76 * c + 76, float(M * c))
    travel("hu", "HU", "HD")
    mm([(T.P4[:, 76 * c:76 * c + 76], T.HB[0:DR, :], T.IB[0:DR, 0:DR], True, True) for c in range(C)], [whole("HB"), whole("IB")], [whole("P4")])
    tt(("MS", 0, 304, 1), ("P4", 0, 304, 1), ("CP", 0, 304, 1), A.is_equal)
    ts(("KJ", 0, 1), ("KI", 0, 1), 15, A.bitwise_and)
    op("v", lambda: g.vector.tensor_tensor_scan(T.SS[:], T.RM[:], T.MS[:], 0.0, A.mult, A.add), [whole("RM"), whole("MS")], [whole("SS")])
    mm([(T.P5[:, 0:304], T.IB[:], T.C336[:], True, False), (T.P5[:, 0:304], T.NTB[:], T.MS[:], False, False),
        (T.P5[:, 0:304], T.BOB[:], T.SS[:], False, True)],
       [whole("IB"), whole("C336"), whole("NTB"), whole("MS"), whole("BOB"), whole("SS")], [whole("P5")])
    copy("v", "KF", 0, 1, "KJ", 0, 1)
    memset("J16", 144, JW, 0.0)
    copy("v", "J16", 16, 144, "J2", 0, 128)
    ts(("LT", 0, 16), ("I16", 0, 16), T.KF[:, 0:1], A.is_gt, [("KF", 0, 1)])
    memset("J16", 0, 16, 0.0)
    tt(("TT", 0, 304, 1), ("P5", 0, 304, 1), ("MS", 0, 304, 1), A.mult)
    tt(("MN", 0, 15, 1), ("LT", 0, 15, 1), ("LT", 1, 16, 1), A.subtract)
    tt(("UU", 0, 152, 1), ("TT", 0, 152, 1), ("TT", 152, 304, 1), A.add)
    op("v", lambda: g.vector.tensor_scalar(T.MR[:, 0:2], T.LT[:, 2:5:2], -1.0, T.LT[:, 6:7], A.mult, A.add), [whole("LT")], [("MR", 0, 2)])
    tt(("SF", 0, 76, 1), ("UU", 0, 76, 1), ("UU", 76, 152, 1), A.add)
    memset("LS0", LC, W0, 0)
    copy("v", "LS1", SU0, SU0 + 76, "SF", 0, 76)
    copy("v", "SH", 0, 76, "SF", 0, 76)
    for i, col in enumerate((("LT", 6), ("LT", 4), ("LT", 2), ("MR", 1), ("MR", 0), ("MN", 6))):
        ts(("SM", JW * i, JW * i + JW), ("J16", 0, JW), T[col[0]][:, col[1]:col[1] + 1], A.mult, [whole(col[0])])
    scatter("NS", 0, C * M, "LS1", SU0, SU0 + 76, "NBI", 0)

    copy("a", "W6", 0, 256, "J2", 0, 256, T.MN[:, 6:7], [whole("MN")])
    for k in range(3):
        lo, hi = BANK * k, min(BANK * k + BANK, V)
        P = T["P%d" % k]
        mm([(P[:, p:hi - lo:16], shifted("J16", 0, 6 - p), T.SH[:, lo // 16:hi // 16], True, True) for p in range(16)],
           [whole("J16"), whole("SH")], [whole("P%d" % k)])
        copy("a", "SR", lo, hi, "P%d" % k, 0, hi - lo)
    gather("a", "HS", 0, "SR", 0, V, "HU", 0, 56)
    mm([(T.P6[:, 0:56], rotated("W6", p - 6), T.HS[:, p:NG:16], p == 0, p == 15) for p in range(16)], [whole("W6"), whole("HS")], [whole("P6")])
    for b in ("Z", "DW", "BW"):
        copy("a", b, 0, Z0, "SC", 0, Z0, 0.0)
    dma("a", T.CW[16 * me:16 * me + E, Z0:ZG], T.co[me], "l_co", w=[whole("CW")])
    for e in range(E):
        copy("a", "BE", 128 * e, 128 * e + 128, "BO", 0, 128, T.MN[:, e:e + 1], [whole("MN")])

    WR = [[(0, 0), (1, 0), (2, 1)], [(2, 3), (3, 0), (4, 0), (5, 2)], [(5, 4), (6, 0), (7, 0)]]

    def wrap(bank, c0, c1):
        P, n = T["P%d" % bank], c1 - c0
        items = []
        for cc, lst in enumerate(WR):
            for i, (a, mk) in enumerate(lst):
                items.append((P[:, cc:LC * n:3], shifted("SM", JW * mk, E * a - 16 * cc), T.NH[:, M * c0 + a:M * c1:8], i == 0, i == len(lst) - 1))
        items += [(P[:, LC * n:LC * n + 21 * n], shifted("SM", JW * 5, p - 6), T.NH[:, M * c0 + p:M * c1:16], p == 0, p == 15) for p in range(16)]
        mm(items, [whole("SM"), ("NH", M * c0, M * c1)], [whole("P%d" % bank)])

    def lists(bank, c0, c1):
        n = c1 - c0
        b, o = nbl("LS", c0)
        ts((b, o, o + LC * n), ("P%d" % bank, 0, LC * n), 1024.0, A.add)
        for c in range(c0, c1):
            i = LC * n + 21 * (c - c0)
            b, o = pul("LS", c)
            op("v", lambda b=b, o=o, i=i: g.vector.tensor_scalar(T[b][:, o:o + 21], T["P%d" % bank][:, i:i + 21], -1.0, 1024.0, A.mult, A.add),
               [("P%d" % bank, i, i + 21)], [(b, o, o + 21)])

    ts(("NH", 0, M), ("NS", 0, M), -1024.0, A.add)
    wrap(3, 0, 1)
    ts(("NH", M, C * M), ("NS", M, C * M), -1024.0, A.add)
    lists(3, 0, 1)
    load_x(0)
    travel("l0", "LS0", "LD0")
    load_x(1)
    wrap(7, 1, C)
    memset("LS1", 3 * LC, SU0, 0)
    memset("SC", 0, BANK, 0.0, E)
    ts(("LS1", HL0, HL0 + 56), ("P6", 0, 56), -1.0, A.mult)
    lists(7, 1, C)
    dma("a", T.D8[0:N, :], T.ld_di[:, d0:d0 + DR, :], "l_di", r=[whole("ld_di")], w=[whole("D8")], after=[("a_di", N - 1)])
    travel("l1", "LS1", "LD1", "a")

    for i, r in enumerate([(me + 1 + e) % N for e in range(N - 1)]):
        dma("a", T.CW[16 * r:16 * r + E, Z0:ZG], T.ld_co[r], "l_co", w=[whole("CW")], after=[("a_co", N - 1)] if i == 0 else [])
    arrive("hu", "HD")
    arrive("l0", "LD0")
    dma("s", T.BW[:, Z0:ZG], T.ld_b[:], "l_b", r=[whole("ld_b")], w=[("BW", Z0, ZG)], after=[("a_b", N - 1)])
    arrive("l1", "LD1")
    for k in range(3):
        lo, hi = BANK * k, min(BANK * k + BANK, V)
        mm([(T["P%d" % k][:, 0:hi - lo], T.E8[0:N, :], T.D8[0:N, lo:hi], True, True)], [whole("E8"), whole("D8")], [whole("P%d" % k)])
        copy("v", "DW", Z0 + lo, Z0 + hi, "P%d" % k, 0, hi - lo)

    ROT = [(7, (0, 1)), (4, (2, 3)), (5, (4, 5)), (6, (6,))]

    def halo_gathers(wb, wlo, whi, lb, l0, qs):
        for q, (a, b) in zip(qs, ((0, 1), (1, 2), (2, 4), (4, 6), (6, 7))):
            gather(q, "HH", G * a, wb, wlo, whi, lb, l0 + 8 * a, l0 + 8 * b)

    def rotate():
        for bank, es in ROT:
            for e in es:
                c0 = G * (max(es) - e)
                mm([(T["P%d" % bank][:, c0:c0 + G], rotated("J2", 16 * (e + 1)), T.HH[:, G * e:G * e + G], True, True)],
                   [whole("J2"), ("HH", G * e, G * e + G)], [("P%d" % bank, c0, c0 + G)])

    def ghost_copies(qs):
        for q, (bank, es) in zip(qs, ROT):
            d = N - 2 - max(es)
            copy(q, "Z", ZG + G * d, ZG + G * (d + len(es)), "P%d" % bank, 0, G * len(es))

    def sort(q, ob, wb, c):
        b, o = pul("LD", c)
        gather(q, ob, M * c, wb, 0, ZG, b, o, o + 21)

    def refill(c, k):
        lo, hi = BANK * k, min(BANK * k + BANK, EM)
        items = []
        for e in range(E):
            j0, j1 = -((e - lo) // E), -((e - hi) // E)
            items.append((T["P%d" % k][:, E * j0 + e - lo:hi - lo:E], T.BE[:, 128 * e:128 * e + 128], T.CS[:, M * c + j0:M * c + j1], True, True))
        mm(items, [whole("BE"), ("CS", M * c, M * c + M)], [whole("P%d" % k)])

    def zgather(q, c, lo, hi):
        b, o = nbl("LD", c)
        gather(q, "ZN", lo, "Z", Z0, ZW, b, o + lo // 16, o + hi // 16)

    def mult(lo, hi):
        k = lo // BANK
        tt(("PR", lo, hi, 1), ("ZN", lo, hi, 1), ("P%d" % k, lo - BANK * k, hi - BANK * k, 1), A.mult)

    def sum_pe(c, k):
        a, b = VCH[k]
        out = T["P%d" % (4 + k)][:, 0:b - a]
        items = [(out, T.J2[:, 0:128], T.PR[:, E * a + e:E * b:E], e == 0, False) for e in range(E)]
        items.append((out, T.IB[:], T.BS[:, M * c + a:M * c + b], False, True))
        mm(items, [whole("J2"), whole("IB"), ("PR", E * a, E * b), ("BS", M * c + a, M * c + b)], [whole("P%d" % (4 + k))])

    def final_pe(c, k):
        a, b = VCH[k]
        tt(("R", M * c + a, M * c + b, 1), ("P%d" % (4 + k), 0, b - a, 1), ("DS", M * c + a, M * c + b, 1), A.mult)

    def sum_scan(c, k):
        a, b = VCH[k]
        n, o = E * (b - a), "P%d" % (4 + k)
        op("v", lambda: g.vector.tensor_tensor_scan(T[o][:, 0:n], T.SC[:, 0:n], T.PR[:, E * a:E * b], 0.0, A.mult, A.add),
           [whole("SC"), ("PR", E * a, E * b)], [(o, 0, n)])
        tt((o, E - 1, n, E), (o, E - 1, n, E), ("BS", M * c + a, M * c + b, 1), A.add)
        tt(("R", M * c + a, M * c + b, 1), (o, E - 1, n, E), ("DS", M * c + a, M * c + b, 1), A.mult)

    halo_gathers("Z", Z0, ZG, "HD", 0, "aaaaa")
    rotate()
    ghost_copies("aaaa")
    sort("v", "CS", "CW", 0)
    for k in range(4):
        refill(0, k)

    for s, c in enumerate(ORDER):
        last = s == len(ORDER) - 1
        nc = ORDER[s + 1] if not last else None
        if s < 2:
            sort("v", "BS", "BW", c)
        for step in (PLAN0 if s < 2 else PLAN):
            if step[0] in "av":
                zgather(step[0], c, step[1], step[2])
            elif step[0] == "m":
                mult(step[1], step[2])
            elif step[0] == "p":
                sum_pe(c, step[1])
            elif step[0] == "s":
                sum_scan(c, step[1])
            elif step[0] == "f":
                final_pe(c, step[1])
            else:
                sort("v", "DS", "DW", c)
        if s < C - 1:
            sort("a", "CS", "CW", nc)
            if s == 0:
                for c2 in range(1, C):
                    sort("a", "R", "Z", c2)
            else:
                sort("a", "BS", "BW", nc)
                sort("a", "DS", "DW", nc)
        if last:
            break
        refill(nc, 0)
        refill(nc, 1)
        halo_gathers("R", 0, C * M, "LD1", HL0, "avaaa")
        b, o = pul("LD", c)
        scatter("Z", 0, ZG, b, o, o + 21, "R", M * c)
        rotate()
        ghost_copies("aava")
        refill(nc, 2)
        refill(nc, 3)

    for k, (a, b, h) in enumerate(YP):
        mid = a // 16 + 2 * ((b - a) // 64)
        gather("v", "Y", a, "R", 0, C * M, "LD1", SU0 + a // 16, SU0 + mid)
        gather("a", "Y", 16 * mid, "R", 0, C * M, "LD1", SU0 + mid, SU0 + b // 16)
        dma("s", T["st_y%d" % k][:], T.Y[:, a:b], "s_y%d" % k, r=[("Y", a, b)], w=[whole("st_y%d" % k)])
        send("y%d" % k, h)
    dma("a", T.y[own, :], T.Y[own, :], "l_own", r=[whole("Y")])
    for k, (a, b, h) in enumerate(YP):
        for i, (r0, r1) in enumerate(around):
            dma("s" if h is None else "a", T.y[16 * r0:16 * r1, a:b], T["ld_y%d" % k][r0:r1], "l_y%d" % k,
                after=[("a_y%d" % k, N - 1)] if i == 0 else [])
    emit(g, T, ops)
